import numpy as np
import ml_dtypes


def mxq(x, axis, fmt="e4m3"):
    dtype, down = {"e4m3": (ml_dtypes.float8_e4m3fn, 7), "e5m2": (ml_dtypes.float8_e5m2, 14)}[fmt]
    v = np.moveaxis(np.asarray(x, np.float32).astype(ml_dtypes.bfloat16).astype(np.float64), axis, -1)
    blocks = v.reshape(v.shape[:-1] + (-1, 32))
    amax = np.abs(blocks).max(-1, keepdims=True)
    byte = np.maximum(np.where(amax > 0, np.frexp(amax)[1] - 1 + 127, 0) - down, 1)
    scale = np.exp2(byte - 127.0)
    codes = (blocks / scale).astype(np.float32).astype(dtype).astype(np.float64)
    return np.moveaxis((codes * scale).reshape(v.shape), -1, axis)


WIDE = False


def mx_kscale(k, group=512):
    if not WIDE:
        return np.ones(k)
    levels = np.array([18, -18])
    if group != 512:
        return np.exp2(np.random.permutation(np.resize(levels, k // group))).repeat(group)
    if k % 512:
        return np.exp2(np.random.permutation(np.resize(levels, k // 32))).repeat(32)
    a = np.empty((k // 512, 16))
    for p in range(k // 512):
        a[p, :8] = np.random.permutation(np.resize(levels, 8))
        for g in range(8):
            far = levels[np.abs(levels - a[p, g]) >= 10]
            a[p, g + 8] = far[np.random.randint(len(far))]
    return np.exp2(a.ravel()).repeat(32)


def f64(x):
    return np.asarray(x).astype(np.float64)


G, D, M, N = 4, 128, 128, 1024


def setup_inputs():
    n = np.random.standard_normal
    s = mx_kscale(D, 0)[:, None]
    return {
        "x": (n((G, D, N)) * s).astype(np.float32),
        "w": (n((G, D, M)) / np.sqrt(D) / s).astype(np.float32),
        "b": (0.5 * n((G, M, 1))).astype(np.float32),
        "r": n((G, M, N)).astype(np.float32),
    }


def reference(x, w, b, r):
    xq = mxq(f64(x), 1, "e4m3")
    y = mxq(f64(w), 1, "e4m3").transpose(0, 2, 1) @ xq
    y = y + f64(b)
    y = np.tanh(y)
    y = y + f64(r)
    return y

@@ -1,0 +1,121 @@
+from contextlib import ExitStack
+
+import concourse.mybir as mybir
+
+G, D, M, N = 4, 128, 128, 1024
+FLOPS = 2 * G * D * M * N
+
+F32 = mybir.dt.float32
+BF16 = mybir.dt.bfloat16
+U32 = mybir.dt.uint32
+U8 = mybir.dt.uint8
+FP8X4 = mybir.dt.float8_e4m3fn_x4
+TANH = mybir.ActivationFunctionType.Tanh
+
+P = 128
+PACK = 4
+ROWS = D // PACK
+HALF = 512
+HALVES = N // HALF
+PAIR = 2
+SCALAR_COLS = (128, 0)
+
+
+def tile_rows_glin_tanh_bias_res_kernel(tc, x, w, b, r, out):
+    nc = tc.nc
+    x_rows = x.rearrange("g (p j) n -> (g p) j n", j=PACK)
+    w_rows = w.rearrange("g (p j) m -> (g p) j m", j=PACK)
+    r_rows = r.rearrange("g m n -> m g n")
+    out_rows = out.rearrange("g m n -> m g n")
+
+    with ExitStack() as ctx:
+        sb = ctx.enter_context(tc.tile_pool(name="sb", bufs=1))
+        ps = ctx.enter_context(tc.psum_pool(name="ps", bufs=1))
+        ctx.enter_context(tc.manual_schedule())
+
+        x_raw = [sb.tile([P, PACK, HALF], F32, name="x_raw%d" % h, align_bytes=64) for h in range(HALVES)]
+        x_bf = [sb.tile([P, HALF, PACK], BF16, name="x_bf%d" % h, align_bytes=64) for h in range(HALVES)]
+        x_codes = [sb.tile([P, HALF], U32, name="x_codes%d" % h, align_bytes=64) for h in range(HALVES)]
+        x_scales = [sb.tile([P, HALF], U8, name="x_scales%d" % h, align_bytes=64) for h in range(HALVES)]
+        w_raw = sb.tile([P, PACK, M], F32, align_bytes=64)
+        w_bf = sb.tile([P, M, PACK], BF16, align_bytes=64)
+        w_codes = sb.tile([P, M], U32, align_bytes=64)
+        w_scales = sb.tile([P, M], U8, align_bytes=64)
+        b_rows = sb.tile([P, G * 32], F32, align_bytes=64)
+        b_cols = sb.tile([P, G * 32], F32, align_bytes=64)
+        warm = sb.tile([P, 8], F32, align_bytes=64)
+        res = [[sb.tile([P, PAIR, HALF], F32, name="res%d_%d" % (h, q), align_bytes=64) for q in range(G // PAIR)] for h in range(1)]
+        act = [[sb.tile([P, HALF], F32, name="act%d_%d" % (h, g), align_bytes=64) for g in range(G)] for h in range(HALVES)]
+        res_last = sb.tile([P, G, HALF], F32, align_bytes=64)
+        acc = [[ps.tile([P, HALF], F32, name="acc%d_%d" % (h, g)) for g in range(G)] for h in range(HALVES)]
+
+        def cols(h):
+            return slice(h * HALF, (h + 1) * HALF)
+
+        def res_view(h, g):
+            if h == 0:
+                return res[0][g // PAIR][:, g % PAIR, :]
+            return res_last[:, g, :]
+
+        nc.gpsimd.memset(b_rows[:], 0.0)
+        nc.gpsimd.memset(warm[:, 0:1], 0.0)
+        nc.sync.dma_start(out=x_raw[0][:], in_=x_rows[:, :, cols(0)])
+        nc.sync.dma_start(out=w_raw[:], in_=w_rows)
+        nc.scalar.dma_start(
+            out=b_rows[0:P:32, :].rearrange("q (g c) -> q g c", g=G),
+            in_=b.rearrange("g (q c) o -> q g (c o)", c=32),
+        )
+        nc.scalar.activation(out=warm[:, 4:5], in_=warm[:, 0:1], func=TANH)
+        nc.sync.dma_start(out=x_raw[1][:], in_=x_rows[:, :, cols(1)])
+        for q in range(G // PAIR):
+            nc.sync.dma_start(out=res[0][q][:], in_=r_rows[:, q * PAIR:(q + 1) * PAIR, cols(0)])
+        nc.sync.dma_start(out=res_last[:], in_=r_rows[:, :, cols(1)])
+
+
+        def interleave(h):
+            split = HALF - SCALAR_COLS[h]
+            nc.vector.tensor_copy(out=x_bf[h][:, :split, :], in_=x_raw[h][:, :, :split].rearrange("p j n -> p n j"))
+            if split < HALF:
+                nc.scalar.copy(out=x_bf[h][:, split:, :], in_=x_raw[h][:, :, split:].rearrange("p j n -> p n j"))
+
+        def quantize(codes, scales, src):
+            nc.vector.quantize_mx(out=codes[:].bitcast(FP8X4), scales=scales[:], in_=src[:].rearrange("p n j -> p (n j)"))
+
+        def multiply(h):
+            for g in range(G):
+                rows = slice(g * ROWS, (g + 1) * ROWS)
+                nc.tensor.matmul_mx(
+                    out=acc[h][g][:],
+                    lhsT=w_codes[rows, :].bitcast(FP8X4),
+                    lhsT_scale=w_scales[rows, :],
+                    rhs=x_codes[h][rows, :].bitcast(FP8X4),
+                    rhs_scale=x_scales[h][rows, :],
+                    start=True,
+                    stop=True,
+                )
+
+        def activate(h):
+            for g in range(G):
+                nc.scalar.activation(out=act[h][g][:], in_=acc[h][g][:], func=TANH, bias=b_cols[:, 32 * g:32 * g + 1])
+
+        def finish(h):
+            for g in range(G):
+                nc.vector.tensor_add(out=res_view(h, g), in0=act[h][g][:], in1=res_view(h, g))
+                if g % PAIR == PAIR - 1:
+                    q = g // PAIR
+                    src = res[0][q][:] if h == 0 else res_last[:, q * PAIR:(q + 1) * PAIR, :]
+                    nc.sync.dma_start(out=out_rows[:, q * PAIR:(q + 1) * PAIR, cols(h)], in_=src)
+
+        interleave(0)
+        nc.scalar.copy(out=w_bf[:], in_=w_raw[:].rearrange("p j m -> p m j"))
+        quantize(x_codes[0], x_scales[0], x_bf[0])
+        quantize(w_codes, w_scales, w_bf)
+        multiply(0)
+        nc.vector.transpose(out=b_cols[:], in_=b_rows[:])
+        interleave(1)
+        activate(0)
+        quantize(x_codes[1], x_scales[1], x_bf[1])
+        multiply(1)
+        activate(1)
+        finish(0)
+        finish(1)

@@ -16,9 +16,11 @@ P = 128
 PACK = 4
 ROWS = D // PACK
 HALF = 512
+QUARTER = 256
 HALVES = N // HALF
-PAIR = 2
-SCALAR_COLS = (128, 0)
+RUN = 4
+SCALAR_COLS = (192, 160)
+PIECES = (((0, 1), (0,)), ((2,), (0, 1)), ((3,), (0, 1)), ((0, 1), (1,)))
 
 
 def tile_rows_glin_tanh_bias_res_kernel(tc, x, w, b, r, out):
@@ -44,78 +46,86 @@ def tile_rows_glin_tanh_bias_res_kernel(tc, x, w, b, r, out):
         b_rows = sb.tile([P, G * 32], F32, align_bytes=64)
         b_cols = sb.tile([P, G * 32], F32, align_bytes=64)
         warm = sb.tile([P, 8], F32, align_bytes=64)
-        res = [[sb.tile([P, PAIR, HALF], F32, name="res%d_%d" % (h, q), align_bytes=64) for q in range(G // PAIR)] for h in range(1)]
+        res = [
+            sb.tile([P, len(groups), len(halves) * HALF], F32, name="res%d" % i, align_bytes=64)
+            for i, (groups, halves) in enumerate(PIECES)
+        ]
         act = [[sb.tile([P, HALF], F32, name="act%d_%d" % (h, g), align_bytes=64) for g in range(G)] for h in range(HALVES)]
-        res_last = sb.tile([P, G, HALF], F32, align_bytes=64)
         acc = [[ps.tile([P, HALF], F32, name="acc%d_%d" % (h, g)) for g in range(G)] for h in range(HALVES)]
 
-        def cols(h):
-            return slice(h * HALF, (h + 1) * HALF)
-
-        def res_view(h, g):
-            if h == 0:
-                return res[0][g // PAIR][:, g % PAIR, :]
-            return res_last[:, g, :]
+        def piece_of(rows, i):
+            groups, halves = PIECES[i]
+            return rows[:, groups[0]:groups[-1] + 1, halves[0] * HALF:(halves[-1] + 1) * HALF]
 
         nc.gpsimd.memset(b_rows[:], 0.0)
         nc.gpsimd.memset(warm[:, 0:1], 0.0)
-        nc.sync.dma_start(out=x_raw[0][:], in_=x_rows[:, :, cols(0)])
-        nc.sync.dma_start(out=w_raw[:], in_=w_rows)
-        nc.scalar.dma_start(
+        nc.scalar.activation(out=warm[:, 4:5], in_=warm[:, 0:1], func=TANH)
+        nc.sync.dma_start(out=x_raw[0][:], in_=x_rows[:, :, 0:HALF])
+        nc.sync.dma_start(
             out=b_rows[0:P:32, :].rearrange("q (g c) -> q g c", g=G),
             in_=b.rearrange("g (q c) o -> q g (c o)", c=32),
         )
-        nc.scalar.activation(out=warm[:, 4:5], in_=warm[:, 0:1], func=TANH)
-        nc.sync.dma_start(out=x_raw[1][:], in_=x_rows[:, :, cols(1)])
-        for q in range(G // PAIR):
-            nc.sync.dma_start(out=res[0][q][:], in_=r_rows[:, q * PAIR:(q + 1) * PAIR, cols(0)])
-        nc.sync.dma_start(out=res_last[:], in_=r_rows[:, :, cols(1)])
+        nc.sync.dma_start(out=w_raw[:], in_=w_rows)
+        nc.sync.dma_start(out=x_raw[1][:], in_=x_rows[:, :, HALF:N])
+        for i in range(len(PIECES)):
+            nc.sync.dma_start(out=res[i][:], in_=piece_of(r_rows, i))
 
+        def interleave(copy, dst, src, lo, hi):
+            copy(
+                out=dst[:, lo:hi, :].rearrange("p (c i) j -> p c j i", i=RUN),
+                in_=src[:, :, lo:hi].rearrange("p j (c i) -> p c j i", i=RUN),
+            )
 
-        def interleave(h):
-            split = HALF - SCALAR_COLS[h]
-            nc.vector.tensor_copy(out=x_bf[h][:, :split, :], in_=x_raw[h][:, :, :split].rearrange("p j n -> p n j"))
-            if split < HALF:
-                nc.scalar.copy(out=x_bf[h][:, split:, :], in_=x_raw[h][:, :, split:].rearrange("p j n -> p n j"))
+        def quantize(codes, scales, src, lo, hi):
+            nc.vector.quantize_mx(
+                out=codes[:, lo:hi].bitcast(FP8X4),
+                scales=scales[:, lo:hi],
+                in_=src[:, lo:hi, :].rearrange("p n j -> p (n j)"),
+            )
 
-        def quantize(codes, scales, src):
-            nc.vector.quantize_mx(out=codes[:].bitcast(FP8X4), scales=scales[:], in_=src[:].rearrange("p n j -> p (n j)"))
+        def multiply(h, g):
+            rows = slice(g * ROWS, (g + 1) * ROWS)
+            nc.tensor.matmul_mx(
+                out=acc[h][g][:],
+                lhsT=w_codes[rows, :].bitcast(FP8X4),
+                lhsT_scale=w_scales[rows, :],
+                rhs=x_codes[h][rows, :].bitcast(FP8X4),
+                rhs_scale=x_scales[h][rows, :],
+                start=True,
+                stop=True,
+            )
 
-        def multiply(h):
-            for g in range(G):
-                rows = slice(g * ROWS, (g + 1) * ROWS)
-                nc.tensor.matmul_mx(
-                    out=acc[h][g][:],
-                    lhsT=w_codes[rows, :].bitcast(FP8X4),
-                    lhsT_scale=w_scales[rows, :],
-                    rhs=x_codes[h][rows, :].bitcast(FP8X4),
-                    rhs_scale=x_scales[h][rows, :],
-                    start=True,
-                    stop=True,
-                )
+        def activate(h, g):
+            nc.scalar.activation(out=act[h][g][:], in_=acc[h][g][:], func=TANH, bias=b_cols[:, 32 * g:32 * g + 1])
 
-        def activate(h):
-            for g in range(G):
-                nc.scalar.activation(out=act[h][g][:], in_=acc[h][g][:], func=TANH, bias=b_cols[:, 32 * g:32 * g + 1])
+        order = [(h, g) for groups, halves in PIECES for g in groups for h in halves]
 
-        def finish(h):
-            for g in range(G):
-                nc.vector.tensor_add(out=res_view(h, g), in0=act[h][g][:], in1=res_view(h, g))
-                if g % PAIR == PAIR - 1:
-                    q = g // PAIR
-                    src = res[0][q][:] if h == 0 else res_last[:, q * PAIR:(q + 1) * PAIR, :]
-                    nc.sync.dma_start(out=out_rows[:, q * PAIR:(q + 1) * PAIR, cols(h)], in_=src)
-
-        interleave(0)
-        nc.scalar.copy(out=w_bf[:], in_=w_raw[:].rearrange("p j m -> p m j"))
-        quantize(x_codes[0], x_scales[0], x_bf[0])
-        quantize(w_codes, w_scales, w_bf)
-        multiply(0)
+        split = HALF - SCALAR_COLS[0]
+        interleave(nc.vector.tensor_copy, x_bf[0], x_raw[0], 0, split)
+        interleave(nc.scalar.copy, x_bf[0], x_raw[0], split, HALF)
+        interleave(nc.scalar.copy, w_bf, w_raw, 0, M)
         nc.vector.transpose(out=b_cols[:], in_=b_rows[:])
-        interleave(1)
-        activate(0)
-        quantize(x_codes[1], x_scales[1], x_bf[1])
-        multiply(1)
-        activate(1)
-        finish(0)
-        finish(1)
+        quantize(x_codes[0], x_scales[0], x_bf[0], 0, HALF)
+        quantize(w_codes, w_scales, w_bf, 0, M)
+        for h, g in order:
+            if h == 0:
+                multiply(h, g)
+
+        split = HALF - SCALAR_COLS[1]
+        interleave(nc.vector.tensor_copy, x_bf[1], x_raw[1], 0, QUARTER)
+        interleave(nc.vector.tensor_copy, x_bf[1], x_raw[1], QUARTER, split)
+        interleave(nc.scalar.copy, x_bf[1], x_raw[1], split, HALF)
+        quantize(x_codes[1], x_scales[1], x_bf[1], 0, QUARTER)
+        quantize(x_codes[1], x_scales[1], x_bf[1], QUARTER, HALF)
+        for h, g in order:
+            if h == 1:
+                multiply(h, g)
+        for h, g in order:
+            activate(h, g)
+
+        for i, (groups, halves) in enumerate(PIECES):
+            for gi, g in enumerate(groups):
+                for hi, h in enumerate(halves):
+                    part = res[i][:, gi, hi * HALF:(hi + 1) * HALF]
+                    nc.vector.tensor_add(out=part, in0=act[h][g][:], in1=part)
+            nc.sync.dma_start(out=piece_of(out_rows, i), in_=res[i][:])

@@ -16,11 +16,11 @@ P = 128
 PACK = 4
 ROWS = D // PACK
 HALF = 512
-QUARTER = 256
 HALVES = N // HALF
 RUN = 4
-SCALAR_COLS = (192, 160)
-PIECES = (((0, 1), (0,)), ((2,), (0, 1)), ((3,), (0, 1)), ((0, 1), (1,)))
+FIRST = 640
+LOADS = (((0, 1), (0,)), ((2,), (0, 1)), ((3,), (0, 1)), ((0, 1), (1,)))
+STORES = (((0, 1), (0,)), ((2,), (0, 1)), ((3,), (0, 1)), ((0, 1), (1,)))
 
 
 def tile_rows_glin_tanh_bias_res_kernel(tc, x, w, b, r, out):
@@ -35,97 +35,99 @@ def tile_rows_glin_tanh_bias_res_kernel(tc, x, w, b, r, out):
         ps = ctx.enter_context(tc.psum_pool(name="ps", bufs=1))
         ctx.enter_context(tc.manual_schedule())
 
-        x_raw = [sb.tile([P, PACK, HALF], F32, name="x_raw%d" % h, align_bytes=64) for h in range(HALVES)]
-        x_bf = [sb.tile([P, HALF, PACK], BF16, name="x_bf%d" % h, align_bytes=64) for h in range(HALVES)]
-        x_codes = [sb.tile([P, HALF], U32, name="x_codes%d" % h, align_bytes=64) for h in range(HALVES)]
-        x_scales = [sb.tile([P, HALF], U8, name="x_scales%d" % h, align_bytes=64) for h in range(HALVES)]
+        x_first = sb.tile([P, PACK, FIRST], F32, align_bytes=64)
+        x_rest = sb.tile([P, PACK, N - FIRST], F32, align_bytes=64)
+        x_bf = sb.tile([P, N, PACK], BF16, align_bytes=64)
+        x_codes = sb.tile([P, N], U32, align_bytes=64)
+        x_scales = sb.tile([P, N], U8, align_bytes=64)
         w_raw = sb.tile([P, PACK, M], F32, align_bytes=64)
         w_bf = sb.tile([P, M, PACK], BF16, align_bytes=64)
         w_codes = sb.tile([P, M], U32, align_bytes=64)
         w_scales = sb.tile([P, M], U8, align_bytes=64)
         b_rows = sb.tile([P, G * 32], F32, align_bytes=64)
         b_cols = sb.tile([P, G * 32], F32, align_bytes=64)
-        warm = sb.tile([P, 8], F32, align_bytes=64)
-        res = [
-            sb.tile([P, len(groups), len(halves) * HALF], F32, name="res%d" % i, align_bytes=64)
-            for i, (groups, halves) in enumerate(PIECES)
-        ]
-        act = [[sb.tile([P, HALF], F32, name="act%d_%d" % (h, g), align_bytes=64) for g in range(G)] for h in range(HALVES)]
+        res = sb.tile([P, G, N], F32, align_bytes=64)
+        act = sb.tile([P, G, N], F32, align_bytes=64)
         acc = [[ps.tile([P, HALF], F32, name="acc%d_%d" % (h, g)) for g in range(G)] for h in range(HALVES)]
 
-        def piece_of(rows, i):
-            groups, halves = PIECES[i]
+        def piece_of(rows, piece):
+            groups, halves = piece
             return rows[:, groups[0]:groups[-1] + 1, halves[0] * HALF:(halves[-1] + 1) * HALF]
 
-        nc.gpsimd.memset(b_rows[:], 0.0)
-        nc.gpsimd.memset(warm[:, 0:1], 0.0)
-        nc.scalar.activation(out=warm[:, 4:5], in_=warm[:, 0:1], func=TANH)
-        nc.sync.dma_start(out=x_raw[0][:], in_=x_rows[:, :, 0:HALF])
+        nc.vector.memset(b_rows[:], 0.0)
+        nc.sync.dma_start(out=x_first[:], in_=x_rows[:, :, 0:FIRST])
         nc.sync.dma_start(
             out=b_rows[0:P:32, :].rearrange("q (g c) -> q g c", g=G),
             in_=b.rearrange("g (q c) o -> q g (c o)", c=32),
         )
         nc.sync.dma_start(out=w_raw[:], in_=w_rows)
-        nc.sync.dma_start(out=x_raw[1][:], in_=x_rows[:, :, HALF:N])
-        for i in range(len(PIECES)):
-            nc.sync.dma_start(out=res[i][:], in_=piece_of(r_rows, i))
+        nc.sync.dma_start(out=x_rest[:], in_=x_rows[:, :, FIRST:N])
+        for piece in LOADS:
+            nc.sync.dma_start(out=piece_of(res, piece), in_=piece_of(r_rows, piece))
 
-        def interleave(copy, dst, src, lo, hi):
+        def interleave(copy, dst, src):
             copy(
-                out=dst[:, lo:hi, :].rearrange("p (c i) j -> p c j i", i=RUN),
-                in_=src[:, :, lo:hi].rearrange("p j (c i) -> p c j i", i=RUN),
+                out=dst.rearrange("p (c i) j -> p c j i", i=RUN),
+                in_=src.rearrange("p j (c i) -> p c j i", i=RUN),
             )
 
-        def quantize(codes, scales, src, lo, hi):
-            nc.vector.quantize_mx(
-                out=codes[:, lo:hi].bitcast(FP8X4),
-                scales=scales[:, lo:hi],
-                in_=src[:, lo:hi, :].rearrange("p n j -> p (n j)"),
-            )
+        def interleave_x(copy, lo, hi):
+            src = x_first[:, :, lo:hi] if hi <= FIRST else x_rest[:, :, lo - FIRST:hi - FIRST]
+            interleave(copy, x_bf[:, lo:hi, :], src)
+
+        def quantize(codes, scales, src):
+            nc.vector.quantize_mx(out=codes.bitcast(FP8X4), scales=scales, in_=src.rearrange("p n j -> p (n j)"))
+
+        def quantize_x(lo, hi):
+            quantize(x_codes[:, lo:hi], x_scales[:, lo:hi], x_bf[:, lo:hi, :])
 
         def multiply(h, g):
             rows = slice(g * ROWS, (g + 1) * ROWS)
+            cols = slice(h * HALF, (h + 1) * HALF)
             nc.tensor.matmul_mx(
                 out=acc[h][g][:],
                 lhsT=w_codes[rows, :].bitcast(FP8X4),
                 lhsT_scale=w_scales[rows, :],
-                rhs=x_codes[h][rows, :].bitcast(FP8X4),
-                rhs_scale=x_scales[h][rows, :],
+                rhs=x_codes[rows, cols].bitcast(FP8X4),
+                rhs_scale=x_scales[rows, cols],
                 start=True,
                 stop=True,
             )
 
         def activate(h, g):
-            nc.scalar.activation(out=act[h][g][:], in_=acc[h][g][:], func=TANH, bias=b_cols[:, 32 * g:32 * g + 1])
+            nc.scalar.activation(
+                out=act[:, g, h * HALF:(h + 1) * HALF], in_=acc[h][g][:], func=TANH, bias=b_cols[:, 32 * g:32 * g + 1]
+            )
 
-        order = [(h, g) for groups, halves in PIECES for g in groups for h in halves]
+        order = [(h, g) for groups, halves in STORES for g in groups for h in halves]
+        on_vector, on_scalar = nc.vector.tensor_copy, nc.scalar.copy
 
-        split = HALF - SCALAR_COLS[0]
-        interleave(nc.vector.tensor_copy, x_bf[0], x_raw[0], 0, split)
-        interleave(nc.scalar.copy, x_bf[0], x_raw[0], split, HALF)
-        interleave(nc.scalar.copy, w_bf, w_raw, 0, M)
+        first_half_only = [h for h, g in order].index(1)
+        interleave_x(on_vector, 0, 256)
+        interleave_x(on_vector, 256, 352)
+        interleave_x(on_scalar, 352, HALF)
+        interleave(on_scalar, w_bf[:], w_raw[:])
+        quantize_x(0, 256)
+        quantize_x(256, HALF)
+        quantize(w_codes[:], w_scales[:], w_bf[:])
+        for h, g in order[:first_half_only]:
+            multiply(h, g)
         nc.vector.transpose(out=b_cols[:], in_=b_rows[:])
-        quantize(x_codes[0], x_scales[0], x_bf[0], 0, HALF)
-        quantize(w_codes, w_scales, w_bf, 0, M)
-        for h, g in order:
-            if h == 0:
-                multiply(h, g)
+        interleave_x(on_scalar, HALF, 640)
 
-        split = HALF - SCALAR_COLS[1]
-        interleave(nc.vector.tensor_copy, x_bf[1], x_raw[1], 0, QUARTER)
-        interleave(nc.vector.tensor_copy, x_bf[1], x_raw[1], QUARTER, split)
-        interleave(nc.scalar.copy, x_bf[1], x_raw[1], split, HALF)
-        quantize(x_codes[1], x_scales[1], x_bf[1], 0, QUARTER)
-        quantize(x_codes[1], x_scales[1], x_bf[1], QUARTER, HALF)
-        for h, g in order:
-            if h == 1:
-                multiply(h, g)
+        interleave_x(on_scalar, 640, 704)
+        interleave_x(on_vector, 704, 768)
+        interleave_x(on_vector, 768, N)
+        quantize_x(HALF, 768)
+        quantize_x(768, N)
+        for h, g in order[first_half_only:]:
+            multiply(h, g)
         for h, g in order:
             activate(h, g)
 
-        for i, (groups, halves) in enumerate(PIECES):
-            for gi, g in enumerate(groups):
-                for hi, h in enumerate(halves):
-                    part = res[i][:, gi, hi * HALF:(hi + 1) * HALF]
-                    nc.vector.tensor_add(out=part, in0=act[h][g][:], in1=part)
-            nc.sync.dma_start(out=piece_of(out_rows, i), in_=res[i][:])
+        for groups, halves in STORES:
+            for g in groups:
+                for h in halves:
+                    part = res[:, g, h * HALF:(h + 1) * HALF]
+                    nc.vector.tensor_add(out=part, in0=act[:, g, h * HALF:(h + 1) * HALF], in1=part)
+            nc.sync.dma_start(out=piece_of(out_rows, (groups, halves)), in_=piece_of(res, (groups, halves)))

from contextlib import ExitStack

import concourse.mybir as mybir

G, D, M, N = 4, 128, 128, 1024
FLOPS = 2 * G * D * M * N

F32 = mybir.dt.float32
BF16 = mybir.dt.bfloat16
U32 = mybir.dt.uint32
U8 = mybir.dt.uint8
FP8X4 = mybir.dt.float8_e4m3fn_x4
TANH = mybir.ActivationFunctionType.Tanh

P = 128
PACK = 4
ROWS = D // PACK
HALF = 512
HALVES = N // HALF
RUN = 4
FIRST = 640
LOADS = (((0, 1), (0,)), ((2,), (0, 1)), ((3,), (0, 1)), ((0, 1), (1,)))
STORES = (((0, 1), (0,)), ((2,), (0, 1)), ((3,), (0, 1)), ((0, 1), (1,)))


def tile_rows_glin_tanh_bias_res_kernel(tc, x, w, b, r, out):
    nc = tc.nc
    x_rows = x.rearrange("g (p j) n -> (g p) j n", j=PACK)
    w_rows = w.rearrange("g (p j) m -> (g p) j m", j=PACK)
    r_rows = r.rearrange("g m n -> m g n")
    out_rows = out.rearrange("g m n -> m g n")

    with ExitStack() as ctx:
        sb = ctx.enter_context(tc.tile_pool(name="sb", bufs=1))
        ps = ctx.enter_context(tc.psum_pool(name="ps", bufs=1))
        ctx.enter_context(tc.manual_schedule())

        x_first = sb.tile([P, PACK, FIRST], F32, align_bytes=64)
        x_rest = sb.tile([P, PACK, N - FIRST], F32, align_bytes=64)
        x_bf = sb.tile([P, N, PACK], BF16, align_bytes=64)
        x_codes = sb.tile([P, N], U32, align_bytes=64)
        x_scales = sb.tile([P, N], U8, align_bytes=64)
        w_raw = sb.tile([P, PACK, M], F32, align_bytes=64)
        w_bf = sb.tile([P, M, PACK], BF16, align_bytes=64)
        w_codes = sb.tile([P, M], U32, align_bytes=64)
        w_scales = sb.tile([P, M], U8, align_bytes=64)
        b_rows = sb.tile([P, G * 32], F32, align_bytes=64)
        b_cols = sb.tile([P, G * 32], F32, align_bytes=64)
        res = sb.tile([P, G, N], F32, align_bytes=64)
        act = sb.tile([P, G, N], F32, align_bytes=64)
        acc = [[ps.tile([P, HALF], F32, name="acc%d_%d" % (h, g)) for g in range(G)] for h in range(HALVES)]

        def piece_of(rows, piece):
            groups, halves = piece
            return rows[:, groups[0]:groups[-1] + 1, halves[0] * HALF:(halves[-1] + 1) * HALF]

        nc.vector.memset(b_rows[:], 0.0)
        nc.sync.dma_start(out=x_first[:], in_=x_rows[:, :, 0:FIRST])
        nc.sync.dma_start(
            out=b_rows[0:P:32, :].rearrange("q (g c) -> q g c", g=G),
            in_=b.rearrange("g (q c) o -> q g (c o)", c=32),
        )
        nc.sync.dma_start(out=w_raw[:], in_=w_rows)
        nc.sync.dma_start(out=x_rest[:], in_=x_rows[:, :, FIRST:N])
        for piece in LOADS:
            nc.sync.dma_start(out=piece_of(res, piece), in_=piece_of(r_rows, piece))

        def interleave(copy, dst, src):
            copy(
                out=dst.rearrange("p (c i) j -> p c j i", i=RUN),
                in_=src.rearrange("p j (c i) -> p c j i", i=RUN),
            )

        def interleave_x(copy, lo, hi):
            src = x_first[:, :, lo:hi] if hi <= FIRST else x_rest[:, :, lo - FIRST:hi - FIRST]
            interleave(copy, x_bf[:, lo:hi, :], src)

        def quantize(codes, scales, src):
            nc.vector.quantize_mx(out=codes.bitcast(FP8X4), scales=scales, in_=src.rearrange("p n j -> p (n j)"))

        def quantize_x(lo, hi):
            quantize(x_codes[:, lo:hi], x_scales[:, lo:hi], x_bf[:, lo:hi, :])

        def multiply(h, g):
            rows = slice(g * ROWS, (g + 1) * ROWS)
            cols = slice(h * HALF, (h + 1) * HALF)
            nc.tensor.matmul_mx(
                out=acc[h][g][:],
                lhsT=w_codes[rows, :].bitcast(FP8X4),
                lhsT_scale=w_scales[rows, :],
                rhs=x_codes[rows, cols].bitcast(FP8X4),
                rhs_scale=x_scales[rows, cols],
                start=True,
                stop=True,
            )

        def activate(h, g):
            nc.scalar.activation(
                out=act[:, g, h * HALF:(h + 1) * HALF], in_=acc[h][g][:], func=TANH, bias=b_cols[:, 32 * g:32 * g + 1]
            )

        order = [(h, g) for groups, halves in STORES for g in groups for h in halves]
        on_vector, on_scalar = nc.vector.tensor_copy, nc.scalar.copy

        first_half_only = [h for h, g in order].index(1)
        interleave_x(on_vector, 0, 256)
        interleave_x(on_vector, 256, 352)
        interleave_x(on_scalar, 352, HALF)
        interleave(on_scalar, w_bf[:], w_raw[:])
        quantize_x(0, 256)
        quantize_x(256, HALF)
        quantize(w_codes[:], w_scales[:], w_bf[:])
        for h, g in order[:first_half_only]:
            multiply(h, g)
        nc.vector.transpose(out=b_cols[:], in_=b_rows[:])
        interleave_x(on_scalar, HALF, 640)

        interleave_x(on_scalar, 640, 704)
        interleave_x(on_vector, 704, 768)
        interleave_x(on_vector, 768, N)
        quantize_x(HALF, 768)
        quantize_x(768, N)
        for h, g in order[first_half_only:]:
            multiply(h, g)
        for h, g in order:
            activate(h, g)

        for groups, halves in STORES:
            for g in groups:
                for h in halves:
                    part = res[:, g, h * HALF:(h + 1) * HALF]
                    nc.vector.tensor_add(out=part, in0=act[:, g, h * HALF:(h + 1) * HALF], in1=part)
            nc.sync.dma_start(out=piece_of(out_rows, (groups, halves)), in_=piece_of(res, (groups, halves)))
